import numpy as np
import ml_dtypes


def mxq(x, axis, fmt="e4m3"):
    dtype, down = {"e4m3": (ml_dtypes.float8_e4m3fn, 7), "e5m2": (ml_dtypes.float8_e5m2, 14)}[fmt]
    v = np.moveaxis(np.asarray(x, np.float32).astype(ml_dtypes.bfloat16).astype(np.float64), axis, -1)
    blocks = v.reshape(v.shape[:-1] + (-1, 32))
    amax = np.abs(blocks).max(-1, keepdims=True)
    byte = np.maximum(np.where(amax > 0, np.frexp(amax)[1] - 1 + 127, 0) - down, 1)
    scale = np.exp2(byte - 127.0)
    codes = (blocks / scale).astype(np.float32).astype(dtype).astype(np.float64)
    return np.moveaxis((codes * scale).reshape(v.shape), -1, axis)


WIDE = False


def mx_kscale(k):
    if not WIDE:
        return np.ones(k)
    levels = np.array([30, -30])
    if k % 512:
        return np.exp2(np.random.permutation(np.resize(levels, k // 32))).repeat(32)
    a = np.empty((k // 512, 16))
    for p in range(k // 512):
        a[p, :8] = np.random.permutation(np.resize(levels, 8))
        for g in range(8):
            far = levels[np.abs(levels - a[p, g]) >= 10]
            a[p, g + 8] = far[np.random.randint(len(far))]
    return np.exp2(a.ravel()).repeat(32)


def f64(x):
    return np.asarray(x).astype(np.float64)


def striped(idx):
    return np.tile(np.asarray(idx).reshape(-1, 16).T, (8, 1)).astype(np.uint16)


def unstriped(offs):
    return offs[:16].T.reshape(-1).astype(np.int64)


E2M1 = np.array([0.0, 0.5, 1.0, 1.5, 2.0, 3.0, 4.0, 6.0, -0.0, -0.5, -1.0, -1.5, -2.0, -3.0, -4.0, -6.0])


def pack_weight(w, fmt):
    k, n = w.shape
    w = f64(np.asarray(w, np.float32).astype(ml_dtypes.bfloat16)).reshape(k // 32, 32, n)
    amax = np.abs(w).max(1)
    if fmt in ("e4m3", "e5m2"):
        byte = np.frexp(amax)[1] - 1 + 127 - (7 if fmt == "e4m3" else 14)
    else:
        mant, ex = np.frexp(amax / 6.0)
        byte = np.where(mant > 0.5, ex, ex - 1) + 127
    byte = np.clip(np.where(amax > 0, byte, 1), 1, 254)
    scaled = (w * np.exp2(127.0 - byte)[:, None, :]).reshape(k, n).astype(np.float32)
    by_word = np.ascontiguousarray(scaled.reshape(k // 512, 128, 4, n).transpose(0, 1, 3, 2))
    if fmt in ("e4m3", "e5m2"):
        words = by_word.astype(ml_dtypes.float8_e4m3fn if fmt == "e4m3" else ml_dtypes.float8_e5m2).view(np.uint8)
    else:
        c = by_word.astype(ml_dtypes.float4_e2m1fn).view(np.uint8) & 0xF
        words = (c[..., 0::2] | (c[..., 1::2] << 4)).reshape(k // 512, 128, 2 * n)
    return np.ascontiguousarray(words), np.ascontiguousarray(byte.astype(np.uint8).reshape(k // 512, 16, n))


def unpack_weight(words, scales, fmt):
    g, _, n = scales.shape
    words = np.ascontiguousarray(words).reshape(g, 128, n, -1)
    if fmt in ("e4m3", "e5m2"):
        vals = words.view(ml_dtypes.float8_e4m3fn if fmt == "e4m3" else ml_dtypes.float8_e5m2).astype(np.float64)
    else:
        nib = np.empty((g, 128, n, 4), np.uint8)
        nib[..., 0::2] = words & 0xF
        nib[..., 1::2] = words >> 4
        vals = E2M1[nib]
    vals = vals * np.repeat(np.exp2(scales.astype(np.float64) - 127.0), 8, axis=1)[..., None]
    return vals.transpose(0, 1, 3, 2).reshape(g * 512, n)


def sigmoid(v):
    return 1.0 / (1.0 + np.exp(-v))


K, T, Z, J, R, C, O, N, E = 512, 1024, 1024, 256, 512, 512, 256, 256, 1024


def setup_inputs():
    n = np.random.standard_normal
    idx = np.random.permutation(T)[:J]
    idx2 = np.random.permutation(Z)[:J]
    idx3 = np.random.permutation(C)[:J]
    idx4 = np.random.permutation(C)[:J]
    idx5 = np.random.permutation(C)[:O]
    idx6 = np.random.permutation(C)[:O]
    idx7 = np.random.permutation(E)[:O]
    fk = mx_kscale(K)
    fr = mx_kscale(R)
    xtp = pack_weight(n((K, T)) / fk[:, None], "e5m2")
    xop = pack_weight(n((K, Z)) / fk[:, None], "e4m3")
    wp = pack_weight(n((K, R)) * 1 / np.sqrt(K) * fk[:, None] * fr, "e2m1")
    w2p = pack_weight(n((K, R)) * 1 / np.sqrt(K) * fk[:, None] * fr, "e5m2")
    wbp = pack_weight(n((R, N)) * 1 / np.sqrt(R) / fr[:, None], "e2m1")
    return {
        "xt_words": xtp[0],
        "xt_scales": xtp[1],
        "xo_words": xop[0],
        "xo_scales": xop[1],
        "w_words": wp[0],
        "w_scales": wp[1],
        "w2_words": w2p[0],
        "w2_scales": w2p[1],
        "wb_words": wbp[0],
        "wb_scales": wbp[1],
        "tz": (n((N, E))).astype(np.float32),
        "so": (np.random.uniform(0.6, 1.6, (N, 1))).astype(np.float32),
        "bo": (np.random.uniform(-1.0, 1.0, (N, 1))).astype(np.float32),
        "offs": striped(idx),
        "offs2": striped(idx2),
        "offs3": striped(idx3),
        "offs4": striped(idx4),
        "offs5": striped(idx5),
        "offs6": striped(idx6),
        "offs7": striped(idx7),
    }


def reference(xt_words, xt_scales, xo_words, xo_scales, w_words, w_scales, w2_words, w2_scales, wb_words, wb_scales, tz, so, bo, offs, offs2, offs3, offs4, offs5, offs6, offs7):
    idx = unstriped(offs)
    idx2 = unstriped(offs2)
    idx3 = unstriped(offs3)
    idx4 = unstriped(offs4)
    idx5 = unstriped(offs5)
    idx6 = unstriped(offs6)
    idx7 = unstriped(offs7)
    xtu = unpack_weight(xt_words, xt_scales, "e5m2")
    xou = unpack_weight(xo_words, xo_scales, "e4m3")
    wu = unpack_weight(w_words, w_scales, "e2m1")
    w2u = unpack_weight(w2_words, w2_scales, "e5m2")
    wbu = unpack_weight(wb_words, wb_scales, "e2m1")
    xtidxg = xtu[:, idx]
    xoidx2g = xou[:, idx2]
    a = wu.T @ xtidxg + w2u.T @ xoidx2g
    b = w2u.T @ xtidxg + wu.T @ xoidx2g
    pw = np.zeros((R, C))
    pw[:, idx3] = a
    pv = np.zeros((R, C))
    pv[:, idx4] = b
    hid = np.abs(pw[:, idx5] - pv[:, idx6])
    hidq = mxq(hid, 0, "e4m3")
    p = wbu.T @ hidq
    y = p * sigmoid(f64(tz)[:, idx7] * f64(so) + f64(bo))
    return y

@@ -1,0 +1,201 @@
+from contextlib import ExitStack
+
+import concourse.mybir as mybir
+
+K, T, Z, J, R, C, O, N, E = 512, 1024, 1024, 256, 512, 512, 256, 256, 1024
+FLOPS = 2 * (4 * K * R * J + R * N * O)
+
+F32 = mybir.dt.float32
+BF16 = mybir.dt.bfloat16
+I32 = mybir.dt.int32
+U32 = mybir.dt.uint32
+U16 = mybir.dt.uint16
+U8 = mybir.dt.uint8
+E4M3 = mybir.dt.float8_e4m3fn_x4
+E5M2 = mybir.dt.float8_e5m2_x4
+E2M1 = mybir.dt.float4_e2m1fn_x4
+ACT = mybir.ActivationFunctionType
+ALU = mybir.AluOpType
+
+P = 128
+PACK = 4
+HALF = O // 2
+LINE = 4
+
+
+def load_scales(queue, plane, scales, quadrants=(0, 1, 2, 3)):
+    for q in quadrants:
+        queue.dma_start(out=plane[32 * q : 32 * q + 4, :].bitcast(I32), in_=scales[0, 4 * q : 4 * q + 4, :].bitcast(I32))
+
+
+def tile_list_crossed_twoboards_one_finalgate_kernel(
+    tc, xt_words, xt_scales, xo_words, xo_scales, w_words, w_scales, w2_words, w2_scales, wb_words, wb_scales,
+    tz, so, bo, offs, offs2, offs3, offs4, offs5, offs6, offs7, out,
+):
+    nc = tc.nc
+    with ExitStack() as ctx:
+        lists = ctx.enter_context(tc.tile_pool(name="lists", bufs=1))
+        keep = ctx.enter_context(tc.tile_pool(name="keep", bufs=1))
+        psum = ctx.enter_context(tc.psum_pool(name="psum", bufs=2))
+
+        def load_list(src, name):
+            tile = lists.tile([P, J // 16], U16, name=name)
+            nc.sync.dma_start(tile[:], src)
+            return tile
+
+        xt_plane = keep.tile([P, T], U8, align_bytes=64)
+        xo_plane = keep.tile([P, Z], U8, align_bytes=64, tag="xo_plane_then_pv")
+        ww_plane = keep.tile([P, 2, R], U8, align_bytes=64, tag="ww_plane_then_pw")
+        wb_plane = keep.tile([P, N], U8, align_bytes=64)
+        nc.gpsimd.memset(xt_plane[:].bitcast(I32), 0)
+        nc.gpsimd.memset(ww_plane[:].rearrange("p a r -> p (a r)").bitcast(I32), 0)
+        nc.gpsimd.memset(xo_plane[:].bitcast(I32), 0)
+        nc.gpsimd.memset(wb_plane[:].bitcast(I32), 0)
+
+        xt_tab = keep.tile([P, T], I32, align_bytes=64, tag="xt_tab_then_tz")
+        xo_tab = keep.tile([P, Z], I32, align_bytes=64, tag="xo_tab_then_tz")
+        w_raw = keep.tile([P, 2 * R], U8, align_bytes=64)
+        w2_raw = keep.tile([P, R], I32, align_bytes=64)
+        l_xt = load_list(offs, "l_xt")
+        l_xo = load_list(offs2, "l_xo")
+        nc.sync.dma_start(out=xt_tab[:], in_=xt_words[0].rearrange("p n t -> p (n t)").bitcast(I32))
+        load_scales(nc.sync, xt_plane, xt_scales, (0, 1, 2, 3,))
+        nc.sync.dma_start(out=w_raw[:].bitcast(I32), in_=w_words[0].bitcast(I32))
+        load_scales(nc.sync, ww_plane[:, 0, :], w_scales, (0, 1,))
+        nc.sync.dma_start(out=w2_raw[:], in_=w2_words[0].rearrange("p n t -> p (n t)").bitcast(I32))
+        load_scales(nc.sync, ww_plane[:, 0, :], w_scales, (2, 3,))
+        load_scales(nc.sync, ww_plane[:, 1, :], w2_scales, (0, 1,))
+        nc.sync.dma_start(out=xo_tab[:], in_=xo_words[0].rearrange("p n t -> p (n t)").bitcast(I32))
+        load_scales(nc.sync, ww_plane[:, 1, :], w2_scales, (2, 3,))
+        load_scales(nc.sync, xo_plane, xo_scales, (0, 1, 2, 3,))
+        l_pw_put = load_list(offs3, "l_pw_put")
+        l_pv_put = load_list(offs4, "l_pv_put")
+        l_pw_get = load_list(offs5, "l_pw_get")
+        l_pv_get = load_list(offs6, "l_pv_get")
+        l_tz = load_list(offs7, "l_tz")
+        wb_codes = keep.tile([P, 2 * N], U8, align_bytes=64)
+        nc.gpsimd.dma_start(out=wb_codes[:].bitcast(I32), in_=wb_words[0].bitcast(I32))
+        load_scales(nc.gpsimd, wb_plane, wb_scales)
+        slope = keep.tile([P, N // P], F32)
+        offset = keep.tile([P, N // P], F32)
+        with nc.allow_non_contiguous_dma(reason="one value a partition"):
+            nc.gpsimd.dma_start(out=slope[:], in_=so.rearrange("(c p) o -> p (c o)", p=P))
+            nc.gpsimd.dma_start(out=offset[:], in_=bo.rearrange("(c p) o -> p (c o)", p=P))
+
+        pw = [keep.tile([P, C], F32, name=f"pw{t}") for t in range(PACK - 1)]
+        pv = [keep.tile([P, C], F32, name=f"pv{t}") for t in range(PACK - 1)]
+        for t in range(PACK - 1):
+            nc.vector.memset(pw[t][:].bitcast(I32), 0)
+            nc.vector.memset(pv[t][:].bitcast(I32), 0)
+
+        xt_codes = keep.tile([P, J], U32, align_bytes=64)
+        xt_sc = keep.tile([P, J], U8, align_bytes=64)
+        xo_codes = keep.tile([P, J], U32, align_bytes=64)
+        xo_sc = keep.tile([P, J], U8, align_bytes=64)
+        w_codes = keep.tile([P, 2 * R], U8, align_bytes=64)
+        w2_codes = keep.tile([P, R], U32, align_bytes=64)
+        ww_sc = keep.tile([P, PACK, 2, P], U8, align_bytes=64)
+
+        def deal_scales(t0, t1):
+            nc.vector.tensor_copy(
+                out=ww_sc[:, t0:t1].rearrange("p t a m -> p a m t"),
+                in_=ww_plane[:].rearrange("p a (m t) -> p a m t", t=PACK)[:, :, :, t0:t1],
+            )
+
+        nc.scalar.copy(
+            out=w_codes[:].bitcast(U16).rearrange("p (t m) -> p m t", t=PACK),
+            in_=w_raw[:].bitcast(U16).rearrange("p (m t) -> p m t", t=PACK),
+        )
+        nc.scalar.copy(
+            out=w2_codes[:].rearrange("p (t m) -> p m t", t=PACK),
+            in_=w2_raw[:].bitcast(U32).rearrange("p (m t) -> p m t", t=PACK),
+        )
+        nc.vector.tensor_copy(xt_codes[:], xt_tab[:].bitcast(U32).indirect(l_xt[:]))
+        nc.vector.tensor_copy(xt_sc[:], xt_plane[:].indirect(l_xt[:]))
+        deal_scales(0, PACK)
+        nc.vector.tensor_copy(xo_codes[:], xo_tab[:].bitcast(U32).indirect(l_xo[:]))
+        nc.vector.tensor_copy(xo_sc[:], xo_plane[:].indirect(l_xo[:]))
+        pw.append(keep.tile([P, C], F32, name="pw_last", align_bytes=64, tag="ww_plane_then_pw"))
+        pv.append(keep.tile([P, C], F32, name="pv_last", align_bytes=64, tag="xo_plane_then_pv"))
+        nc.vector.memset(pv[-1][:].bitcast(I32), 0)
+        nc.vector.memset(pw[-1][:].bitcast(I32), 0)
+        tz_rows = []
+        for c, tag in enumerate(("xt_tab_then_tz", "xo_tab_then_tz")):
+            rows = keep.tile([P, E], F32, name=f"tz_rows{c}", align_bytes=64, tag=tag)
+            nc.sync.dma_start(out=rows[:], in_=tz[c * P : (c + 1) * P, :])
+            tz_rows.append(rows)
+
+        def product(acc, t, first_is_w):
+            w_side = (w_codes[:, 2 * P * t : 2 * P * (t + 1)].bitcast(E2M1), ww_sc[:, t, 0, :])
+            w2_side = (w2_codes[:, P * t : P * (t + 1)].bitcast(E5M2), ww_sc[:, t, 1, :])
+            on_xt, on_xo = (w_side, w2_side) if first_is_w else (w2_side, w_side)
+            nc.tensor.matmul_mx(out=acc[:], lhsT=on_xt[0], lhsT_scale=on_xt[1],
+                                rhs=xt_codes[:].bitcast(E5M2), rhs_scale=xt_sc[:], start=True, stop=False)
+            nc.tensor.matmul_mx(out=acc[:], lhsT=on_xo[0], lhsT_scale=on_xo[1],
+                                rhs=xo_codes[:].bitcast(E4M3), rhs_scale=xo_sc[:], start=False, stop=True)
+
+        a_acc, b_acc = [], []
+        for t in range(PACK):
+            a_acc.append(psum.tile([P, J], F32, name="a_acc", bufs=PACK))
+            b_acc.append(psum.tile([P, J], F32, name="b_acc", bufs=PACK))
+            product(a_acc[t], t, True)
+            product(b_acc[t], t, False)
+
+        a_sb = [keep.tile([P, J], F32, name=f"a_sb{t}") for t in range(PACK)]
+        b_sb = [keep.tile([P, J], F32, name=f"b_sb{t}") for t in range(PACK)]
+        pw_read = keep.tile([P, PACK, O], F32)
+
+        def put(t):
+            nc.scalar.copy(out=a_sb[t][:], in_=a_acc[t][:])
+            if t == -9 - 1:
+                nc.scalar.copy(out=b_sb[t + 1][:], in_=b_acc[t + 1][:])
+            if t != -9:
+                nc.vector.tensor_copy(out=b_sb[t][:], in_=b_acc[t][:])
+            nc.scalar.activation(out=pw[t][:].indirect(l_pw_put[:]), in_=a_sb[t][:], func=ACT.Copy)
+            nc.vector.tensor_copy(out=pv[t][:].indirect(l_pv_put[:]), in_=b_sb[t][:])
+            nc.scalar.activation(out=pw_read[:, t, :], in_=pw[t][:].indirect(l_pw_get[:]), func=ACT.Copy)
+
+        def subtract(t, o0, o1):
+            nc.vector.tensor_tensor(diff[:, t, o0:o1], pv[t][:].indirect(l_pv_get[:, o0 // 16 : o1 // 16]),
+                                    pw_read[:, t, o0:o1], ALU.subtract)
+
+        put(0)
+        put(1)
+        diff = keep.tile([P, PACK, O], F32, tag="b_sb1")
+        subtract(0, 0, O)
+        for t in range(2, PACK):
+            put(t)
+            subtract(t - 1, 0, O)
+
+        def make_gate(c, tag):
+            gate = keep.tile([P, O], F32, name=f"gate{c}", tag=tag)
+            nc.scalar.activation(out=gate[:], in_=tz_rows[c][:].indirect(l_tz[:]), func=ACT.Sigmoid,
+                                 bias=offset[:, c : c + 1], scale=slope[:, c : c + 1])
+            return gate
+
+        gates = [make_gate(0, "a_sb3")]
+        hid = []
+        for h in range(2):
+            subtract(PACK - 1, h * HALF, (h + 1) * HALF)
+            hid_h = keep.tile([P, HALF * PACK], BF16, name=f"hid{h}", align_bytes=64)
+            nc.scalar.activation(
+                out=hid_h[:].rearrange("p (c i t) -> p c t i", i=LINE, t=PACK),
+                in_=diff[:, :, h * HALF : (h + 1) * HALF].rearrange("p t (c i) -> p c t i", i=LINE),
+                func=ACT.Abs,
+            )
+            hid.append(hid_h)
+        gates.append(make_gate(1, "b_sb1"))
+        p_acc = [psum.tile([P, O], F32, name="a_acc", bufs=PACK) for c in range(N // P)]
+        for h in range(2):
+            hid_codes = keep.tile([P, HALF], U32, name=f"hid_codes{h}", align_bytes=64)
+            hid_sc = keep.tile([P, HALF], U8, name=f"hid_sc{h}", align_bytes=64)
+            nc.vector.quantize_mx(out=hid_codes[:].bitcast(E4M3), scales=hid_sc[:], in_=hid[h][:])
+            for c in range(N // P):
+                nc.tensor.matmul_mx(out=p_acc[c][:, h * HALF : (h + 1) * HALF],
+                                    lhsT=wb_codes[:, 2 * P * c : 2 * P * (c + 1)].bitcast(E2M1),
+                                    lhsT_scale=wb_plane[:, P * c : P * (c + 1)],
+                                    rhs=hid_codes[:].bitcast(E4M3), rhs_scale=hid_sc[:], start=True, stop=True)
+        for c in range(N // P):
+            y = keep.tile([P, O], F32, name=f"y{c}")
+            nc.vector.tensor_tensor(y[:], p_acc[c][:], gates[c][:], ALU.mult)
+            nc.sync.dma_start(out=out[c * P : (c + 1) * P, :], in_=y[:])

@@ -51,6 +51,10 @@ def tile_list_crossed_twoboards_one_finalgate_kernel(
         nc.gpsimd.memset(ww_plane[:].rearrange("p a r -> p (a r)").bitcast(I32), 0)
         nc.gpsimd.memset(xo_plane[:].bitcast(I32), 0)
         nc.gpsimd.memset(wb_plane[:].bitcast(I32), 0)
+        warm_in = keep.tile([P, 1], F32)
+        warm_out = keep.tile([P, 1], F32)
+        nc.gpsimd.memset(warm_in[:], 0.0)
+        nc.scalar.activation(out=warm_out[:], in_=warm_in[:], func=ACT.Sigmoid)
 
         xt_tab = keep.tile([P, T], I32, align_bytes=64, tag="xt_tab_then_tz")
         xo_tab = keep.tile([P, Z], I32, align_bytes=64, tag="xo_tab_then_tz")

@@ -44,12 +44,12 @@ def tile_list_crossed_twoboards_one_finalgate_kernel(
             return tile
 
         xt_plane = keep.tile([P, T], U8, align_bytes=64)
-        xo_plane = keep.tile([P, Z], U8, align_bytes=64, tag="xo_plane_then_pv")
-        ww_plane = keep.tile([P, 2, R], U8, align_bytes=64, tag="ww_plane_then_pw")
+        xo_plane = keep.tile([P, Z], U8, align_bytes=64)
+        ww_plane = keep.tile([P, 2, R], U8, align_bytes=64)
         wb_plane = keep.tile([P, N], U8, align_bytes=64)
         nc.gpsimd.memset(xt_plane[:].bitcast(I32), 0)
-        nc.gpsimd.memset(ww_plane[:].rearrange("p a r -> p (a r)").bitcast(I32), 0)
-        nc.gpsimd.memset(xo_plane[:].bitcast(I32), 0)
+        nc.vector.memset(xo_plane[:].bitcast(I32), 0)
+        nc.vector.memset(ww_plane[:].rearrange("p a r -> p (a r)").bitcast(I32), 0)
         nc.gpsimd.memset(wb_plane[:].bitcast(I32), 0)
         warm_in = keep.tile([P, 1], F32)
         warm_out = keep.tile([P, 1], F32)
@@ -62,35 +62,32 @@ def tile_list_crossed_twoboards_one_finalgate_kernel(
         w2_raw = keep.tile([P, R], I32, align_bytes=64)
         l_xt = load_list(offs, "l_xt")
         l_xo = load_list(offs2, "l_xo")
-        nc.sync.dma_start(out=xt_tab[:], in_=xt_words[0].rearrange("p n t -> p (n t)").bitcast(I32))
         load_scales(nc.sync, xt_plane, xt_scales, (0, 1, 2, 3,))
-        nc.sync.dma_start(out=w_raw[:].bitcast(I32), in_=w_words[0].bitcast(I32))
-        load_scales(nc.sync, ww_plane[:, 0, :], w_scales, (0, 1,))
+        nc.gpsimd.dma_start(out=w_raw[:].bitcast(I32), in_=w_words[0].bitcast(I32))
         nc.sync.dma_start(out=w2_raw[:], in_=w2_words[0].rearrange("p n t -> p (n t)").bitcast(I32))
-        load_scales(nc.sync, ww_plane[:, 0, :], w_scales, (2, 3,))
-        load_scales(nc.sync, ww_plane[:, 1, :], w2_scales, (0, 1,))
-        nc.sync.dma_start(out=xo_tab[:], in_=xo_words[0].rearrange("p n t -> p (n t)").bitcast(I32))
-        load_scales(nc.sync, ww_plane[:, 1, :], w2_scales, (2, 3,))
+        nc.sync.dma_start(out=xt_tab[:], in_=xt_words[0].rearrange("p n t -> p (n t)").bitcast(I32))
         load_scales(nc.sync, xo_plane, xo_scales, (0, 1, 2, 3,))
+        load_scales(nc.sync, ww_plane[:, 0, :], w_scales, (0, 1,))
+        nc.sync.dma_start(out=xo_tab[:], in_=xo_words[0].rearrange("p n t -> p (n t)").bitcast(I32))
+        load_scales(nc.sync, ww_plane[:, 0, :], w_scales, (2, 3,))
+        load_scales(nc.sync, ww_plane[:, 1, :], w2_scales, (0, 1, 2, 3,))
         l_pw_put = load_list(offs3, "l_pw_put")
         l_pv_put = load_list(offs4, "l_pv_put")
         l_pw_get = load_list(offs5, "l_pw_get")
         l_pv_get = load_list(offs6, "l_pv_get")
         l_tz = load_list(offs7, "l_tz")
-        wb_codes = keep.tile([P, 2 * N], U8, align_bytes=64)
-        nc.gpsimd.dma_start(out=wb_codes[:].bitcast(I32), in_=wb_words[0].bitcast(I32))
-        load_scales(nc.gpsimd, wb_plane, wb_scales)
         slope = keep.tile([P, N // P], F32)
         offset = keep.tile([P, N // P], F32)
         with nc.allow_non_contiguous_dma(reason="one value a partition"):
-            nc.gpsimd.dma_start(out=slope[:], in_=so.rearrange("(c p) o -> p (c o)", p=P))
-            nc.gpsimd.dma_start(out=offset[:], in_=bo.rearrange("(c p) o -> p (c o)", p=P))
+            nc.sync.dma_start(out=slope[:], in_=so.rearrange("(c p) o -> p (c o)", p=P))
+            nc.sync.dma_start(out=offset[:], in_=bo.rearrange("(c p) o -> p (c o)", p=P))
 
-        pw = [keep.tile([P, C], F32, name=f"pw{t}") for t in range(PACK - 1)]
-        pv = [keep.tile([P, C], F32, name=f"pv{t}") for t in range(PACK - 1)]
-        for t in range(PACK - 1):
-            nc.vector.memset(pw[t][:].bitcast(I32), 0)
-            nc.vector.memset(pv[t][:].bitcast(I32), 0)
+        pw = [keep.tile([P, C], F32, name=f"pw{t}") for t in range(PACK)]
+        pv = [keep.tile([P, C], F32, name=f"pv{t}") for t in range(PACK)]
+        for t in range(PACK):
+            engine = nc.vector if t < PACK // 2 else nc.gpsimd
+            engine.memset(pw[t][:].bitcast(I32), 0)
+            engine.memset(pv[t][:].bitcast(I32), 0)
 
         xt_codes = keep.tile([P, J], U32, align_bytes=64)
         xt_sc = keep.tile([P, J], U8, align_bytes=64)
@@ -116,18 +113,19 @@ def tile_list_crossed_twoboards_one_finalgate_kernel(
         )
         nc.vector.tensor_copy(xt_codes[:], xt_tab[:].bitcast(U32).indirect(l_xt[:]))
         nc.vector.tensor_copy(xt_sc[:], xt_plane[:].indirect(l_xt[:]))
-        deal_scales(0, PACK)
-        nc.vector.tensor_copy(xo_codes[:], xo_tab[:].bitcast(U32).indirect(l_xo[:]))
         nc.vector.tensor_copy(xo_sc[:], xo_plane[:].indirect(l_xo[:]))
-        pw.append(keep.tile([P, C], F32, name="pw_last", align_bytes=64, tag="ww_plane_then_pw"))
-        pv.append(keep.tile([P, C], F32, name="pv_last", align_bytes=64, tag="xo_plane_then_pv"))
-        nc.vector.memset(pv[-1][:].bitcast(I32), 0)
-        nc.vector.memset(pw[-1][:].bitcast(I32), 0)
+        nc.vector.tensor_copy(xo_codes[:], xo_tab[:].bitcast(U32).indirect(l_xo[:]))
+        deal_scales(0, 1)
+        deal_scales(1, PACK)
         tz_rows = []
         for c, tag in enumerate(("xt_tab_then_tz", "xo_tab_then_tz")):
             rows = keep.tile([P, E], F32, name=f"tz_rows{c}", align_bytes=64, tag=tag)
             nc.sync.dma_start(out=rows[:], in_=tz[c * P : (c + 1) * P, :])
             tz_rows.append(rows)
+
+        wb_codes = keep.tile([P, 2 * N], U8, align_bytes=64)
+        nc.sync.dma_start(out=wb_codes[:].bitcast(I32), in_=wb_words[0].bitcast(I32))
+        load_scales(nc.sync, wb_plane, wb_scales)
 
         def product(acc, t, first_is_w):
             w_side = (w_codes[:, 2 * P * t : 2 * P * (t + 1)].bitcast(E2M1), ww_sc[:, t, 0, :])
@@ -138,38 +136,34 @@ def tile_list_crossed_twoboards_one_finalgate_kernel(
             nc.tensor.matmul_mx(out=acc[:], lhsT=on_xo[0], lhsT_scale=on_xo[1],
                                 rhs=xo_codes[:].bitcast(E4M3), rhs_scale=xo_sc[:], start=False, stop=True)
 
-        a_acc, b_acc = [], []
-        for t in range(PACK):
-            a_acc.append(psum.tile([P, J], F32, name="a_acc", bufs=PACK))
-            b_acc.append(psum.tile([P, J], F32, name="b_acc", bufs=PACK))
-            product(a_acc[t], t, True)
-            product(b_acc[t], t, False)
-
-        a_sb = [keep.tile([P, J], F32, name=f"a_sb{t}") for t in range(PACK)]
-        b_sb = [keep.tile([P, J], F32, name=f"b_sb{t}") for t in range(PACK)]
         pw_read = keep.tile([P, PACK, O], F32)
+        last = PACK - 1
+        halves = [(h * HALF, (h + 1) * HALF) for h in range(2)]
 
-        def put(t):
-            nc.scalar.copy(out=a_sb[t][:], in_=a_acc[t][:])
-            if t == -9 - 1:
-                nc.scalar.copy(out=b_sb[t + 1][:], in_=b_acc[t + 1][:])
-            if t != -9:
-                nc.vector.tensor_copy(out=b_sb[t][:], in_=b_acc[t][:])
-            nc.scalar.activation(out=pw[t][:].indirect(l_pw_put[:]), in_=a_sb[t][:], func=ACT.Copy)
-            nc.vector.tensor_copy(out=pv[t][:].indirect(l_pv_put[:]), in_=b_sb[t][:])
+        def read_pw(t):
             nc.scalar.activation(out=pw_read[:, t, :], in_=pw[t][:].indirect(l_pw_get[:]), func=ACT.Copy)
 
         def subtract(t, o0, o1):
             nc.vector.tensor_tensor(diff[:, t, o0:o1], pv[t][:].indirect(l_pv_get[:, o0 // 16 : o1 // 16]),
                                     pw_read[:, t, o0:o1], ALU.subtract)
 
-        put(0)
-        put(1)
-        diff = keep.tile([P, PACK, O], F32, tag="b_sb1")
-        subtract(0, 0, O)
-        for t in range(2, PACK):
-            put(t)
-            subtract(t - 1, 0, O)
+        for t in range(PACK):
+            a_acc = psum.tile([P, J], F32, name="a_acc")
+            b_acc = psum.tile([P, J], F32, name="b_acc")
+            product(a_acc, t, True)
+            product(b_acc, t, False)
+            a_sb = keep.tile([P, J], F32, name=f"a_sb{t}")
+            b_sb = keep.tile([P, J], F32, name=f"b_sb{t}")
+            nc.vector.tensor_copy(out=a_sb[:], in_=a_acc[:])
+            nc.scalar.copy(out=b_sb[:], in_=b_acc[:])
+            if t >= 1:
+                read_pw(t - 1)
+            if t == 2:
+                diff = keep.tile([P, PACK, O], F32, tag="b_sb1")
+            if t >= 2:
+                subtract(t - 2, 0, O)
+            nc.scalar.activation(out=pw[t][:].indirect(l_pw_put[:]), in_=a_sb[:], func=ACT.Copy)
+            nc.vector.tensor_copy(out=pv[t][:].indirect(l_pv_put[:]), in_=b_sb[:])
 
         def make_gate(c, tag):
             gate = keep.tile([P, O], F32, name=f"gate{c}", tag=tag)
@@ -177,29 +171,34 @@ def tile_list_crossed_twoboards_one_finalgate_kernel(
                                  bias=offset[:, c : c + 1], scale=slope[:, c : c + 1])
             return gate
 
-        gates = [make_gate(0, "a_sb3")]
-        hid = []
-        for h in range(2):
-            subtract(PACK - 1, h * HALF, (h + 1) * HALF)
-            hid_h = keep.tile([P, HALF * PACK], BF16, name=f"hid{h}", align_bytes=64)
-            nc.scalar.activation(
-                out=hid_h[:].rearrange("p (c i t) -> p c t i", i=LINE, t=PACK),
-                in_=diff[:, :, h * HALF : (h + 1) * HALF].rearrange("p t (c i) -> p c t i", i=LINE),
-                func=ACT.Abs,
-            )
-            hid.append(hid_h)
+        mag = keep.tile([P, PACK, O], BF16, tag=f"a_sb{last}")
+        nc.scalar.activation(out=mag[:, : last - 1, :], in_=diff[:, : last - 1, :], func=ACT.Abs)
+        subtract(last - 1, 0, O)
+        nc.scalar.activation(out=mag[:, last - 1, :], in_=diff[:, last - 1, :], func=ACT.Abs)
+        for o0, o1 in halves:
+            nc.vector.tensor_copy(pw_read[:, last, o0:o1], pw[last][:].indirect(l_pw_get[:, o0 // 16 : o1 // 16]))
+        gates = [make_gate(0, f"b_sb{last}")]
+        for o0, o1 in halves:
+            subtract(last, o0, o1)
+            nc.scalar.activation(out=mag[:, last, o0:o1], in_=diff[:, last, o0:o1], func=ACT.Abs)
         gates.append(make_gate(1, "b_sb1"))
-        p_acc = [psum.tile([P, O], F32, name="a_acc", bufs=PACK) for c in range(N // P)]
-        for h in range(2):
+        hid = []
+        for h, (o0, o1) in enumerate(halves):
+            hid_h = keep.tile([P, HALF * PACK], BF16, name=f"hid{h}", align_bytes=64)
+            nc.vector.tensor_copy(out=hid_h[:].rearrange("p (o t) -> p o t", t=PACK),
+                                  in_=mag[:, :, o0:o1].rearrange("p t o -> p o t"))
+            hid.append(hid_h)
+        out_rows = out.rearrange("(c p) o -> p c o", p=P)
+        for h, (o0, o1) in enumerate(halves):
             hid_codes = keep.tile([P, HALF], U32, name=f"hid_codes{h}", align_bytes=64)
             hid_sc = keep.tile([P, HALF], U8, name=f"hid_sc{h}", align_bytes=64)
             nc.vector.quantize_mx(out=hid_codes[:].bitcast(E4M3), scales=hid_sc[:], in_=hid[h][:])
+            p_acc = psum.tile([P, N // P, HALF], F32, name="p_acc")
             for c in range(N // P):
-                nc.tensor.matmul_mx(out=p_acc[c][:, h * HALF : (h + 1) * HALF],
-                                    lhsT=wb_codes[:, 2 * P * c : 2 * P * (c + 1)].bitcast(E2M1),
+                nc.tensor.matmul_mx(out=p_acc[:, c, :], lhsT=wb_codes[:, 2 * P * c : 2 * P * (c + 1)].bitcast(E2M1),
                                     lhsT_scale=wb_plane[:, P * c : P * (c + 1)],
                                     rhs=hid_codes[:].bitcast(E4M3), rhs_scale=hid_sc[:], start=True, stop=True)
-        for c in range(N // P):
-            y = keep.tile([P, O], F32, name=f"y{c}")
-            nc.vector.tensor_tensor(y[:], p_acc[c][:], gates[c][:], ALU.mult)
-            nc.sync.dma_start(out=out[c * P : (c + 1) * P, :], in_=y[:])
+            y = keep.tile([P, N // P, HALF], F32, name=f"y{h}")
+            for c in range(N // P):
+                nc.vector.tensor_tensor(y[:, c, :], p_acc[:, c, :], gates[c][:, o0:o1], ALU.mult)
+            nc.sync.dma_start(out=out_rows[:, :, o0:o1], in_=y[:])

@@ -45,11 +45,13 @@ def tile_list_crossed_twoboards_one_finalgate_kernel(
 
         xt_plane = keep.tile([P, T], U8, align_bytes=64)
         xo_plane = keep.tile([P, Z], U8, align_bytes=64)
-        ww_plane = keep.tile([P, 2, R], U8, align_bytes=64)
+        w_plane = keep.tile([P, R], U8, align_bytes=64)
+        w2_plane = keep.tile([P, R], U8, align_bytes=64)
         wb_plane = keep.tile([P, N], U8, align_bytes=64)
         nc.gpsimd.memset(xt_plane[:].bitcast(I32), 0)
         nc.vector.memset(xo_plane[:].bitcast(I32), 0)
-        nc.vector.memset(ww_plane[:].rearrange("p a r -> p (a r)").bitcast(I32), 0)
+        nc.gpsimd.memset(w_plane[:].bitcast(I32), 0)
+        nc.vector.memset(w2_plane[:].bitcast(I32), 0)
         nc.gpsimd.memset(wb_plane[:].bitcast(I32), 0)
         warm_in = keep.tile([P, 1], F32)
         warm_out = keep.tile([P, 1], F32)
@@ -63,14 +65,15 @@ def tile_list_crossed_twoboards_one_finalgate_kernel(
         l_xt = load_list(offs, "l_xt")
         l_xo = load_list(offs2, "l_xo")
         load_scales(nc.sync, xt_plane, xt_scales, (0, 1, 2, 3,))
+        load_scales(nc.sync, w_plane, w_scales, (0,))
         nc.gpsimd.dma_start(out=w_raw[:].bitcast(I32), in_=w_words[0].bitcast(I32))
-        nc.sync.dma_start(out=w2_raw[:], in_=w2_words[0].rearrange("p n t -> p (n t)").bitcast(I32))
+        load_scales(nc.gpsimd, w_plane, w_scales, (3,))
         nc.sync.dma_start(out=xt_tab[:], in_=xt_words[0].rearrange("p n t -> p (n t)").bitcast(I32))
-        load_scales(nc.sync, xo_plane, xo_scales, (0, 1, 2, 3,))
-        load_scales(nc.sync, ww_plane[:, 0, :], w_scales, (0, 1,))
+        load_scales(nc.sync, xo_plane, xo_scales)
+        load_scales(nc.sync, w_plane, w_scales, (1, 2))
         nc.sync.dma_start(out=xo_tab[:], in_=xo_words[0].rearrange("p n t -> p (n t)").bitcast(I32))
-        load_scales(nc.sync, ww_plane[:, 0, :], w_scales, (2, 3,))
-        load_scales(nc.sync, ww_plane[:, 1, :], w2_scales, (0, 1, 2, 3,))
+        nc.sync.dma_start(out=w2_raw[:], in_=w2_words[0].rearrange("p n t -> p (n t)").bitcast(I32))
+        load_scales(nc.sync, w2_plane, w2_scales, (0, 1, 2, 3,))
         l_pw_put = load_list(offs3, "l_pw_put")
         l_pv_put = load_list(offs4, "l_pv_put")
         l_pw_get = load_list(offs5, "l_pw_get")
@@ -85,7 +88,7 @@ def tile_list_crossed_twoboards_one_finalgate_kernel(
         pw = [keep.tile([P, C], F32, name=f"pw{t}") for t in range(PACK)]
         pv = [keep.tile([P, C], F32, name=f"pv{t}") for t in range(PACK)]
         for t in range(PACK):
-            engine = nc.vector if t < PACK // 2 else nc.gpsimd
+            engine = nc.vector if t == 0 else nc.gpsimd
             engine.memset(pw[t][:].bitcast(I32), 0)
             engine.memset(pv[t][:].bitcast(I32), 0)
 
@@ -95,28 +98,31 @@ def tile_list_crossed_twoboards_one_finalgate_kernel(
         xo_sc = keep.tile([P, J], U8, align_bytes=64)
         w_codes = keep.tile([P, 2 * R], U8, align_bytes=64)
         w2_codes = keep.tile([P, R], U32, align_bytes=64)
-        ww_sc = keep.tile([P, PACK, 2, P], U8, align_bytes=64)
+        w_sc = keep.tile([P, PACK, P], U8, align_bytes=64)
+        w2_sc = keep.tile([P, PACK, P], U8, align_bytes=64)
 
-        def deal_scales(t0, t1):
+        def deal_scales(dealt, plane, t0, t1):
             nc.vector.tensor_copy(
-                out=ww_sc[:, t0:t1].rearrange("p t a m -> p a m t"),
-                in_=ww_plane[:].rearrange("p a (m t) -> p a m t", t=PACK)[:, :, :, t0:t1],
+                out=dealt[:, t0:t1, :].rearrange("p t m -> p m t"),
+                in_=plane[:].rearrange("p (m t) -> p m t", t=PACK)[:, :, t0:t1],
             )
 
         nc.scalar.copy(
             out=w_codes[:].bitcast(U16).rearrange("p (t m) -> p m t", t=PACK),
             in_=w_raw[:].bitcast(U16).rearrange("p (m t) -> p m t", t=PACK),
         )
-        nc.scalar.copy(
-            out=w2_codes[:].rearrange("p (t m) -> p m t", t=PACK),
-            in_=w2_raw[:].bitcast(U32).rearrange("p (m t) -> p m t", t=PACK),
-        )
+        for t0, t1 in ((0, 1), (1, PACK)):
+            nc.scalar.copy(
+                out=w2_codes[:].rearrange("p (t m) -> p m t", t=PACK)[:, :, t0:t1],
+                in_=w2_raw[:].bitcast(U32).rearrange("p (m t) -> p m t", t=PACK)[:, :, t0:t1],
+            )
         nc.vector.tensor_copy(xt_codes[:], xt_tab[:].bitcast(U32).indirect(l_xt[:]))
         nc.vector.tensor_copy(xt_sc[:], xt_plane[:].indirect(l_xt[:]))
         nc.vector.tensor_copy(xo_sc[:], xo_plane[:].indirect(l_xo[:]))
+        deal_scales(w_sc, w_plane, 0, PACK)
         nc.vector.tensor_copy(xo_codes[:], xo_tab[:].bitcast(U32).indirect(l_xo[:]))
-        deal_scales(0, 1)
-        deal_scales(1, PACK)
+        deal_scales(w2_sc, w2_plane, 0, 1)
+        deal_scales(w2_sc, w2_plane, 1, PACK)
         tz_rows = []
         for c, tag in enumerate(("xt_tab_then_tz", "xo_tab_then_tz")):
             rows = keep.tile([P, E], F32, name=f"tz_rows{c}", align_bytes=64, tag=tag)
@@ -127,14 +133,14 @@ def tile_list_crossed_twoboards_one_finalgate_kernel(
         nc.sync.dma_start(out=wb_codes[:].bitcast(I32), in_=wb_words[0].bitcast(I32))
         load_scales(nc.sync, wb_plane, wb_scales)
 
-        def product(acc, t, first_is_w):
-            w_side = (w_codes[:, 2 * P * t : 2 * P * (t + 1)].bitcast(E2M1), ww_sc[:, t, 0, :])
-            w2_side = (w2_codes[:, P * t : P * (t + 1)].bitcast(E5M2), ww_sc[:, t, 1, :])
-            on_xt, on_xo = (w_side, w2_side) if first_is_w else (w2_side, w_side)
-            nc.tensor.matmul_mx(out=acc[:], lhsT=on_xt[0], lhsT_scale=on_xt[1],
-                                rhs=xt_codes[:].bitcast(E5M2), rhs_scale=xt_sc[:], start=True, stop=False)
-            nc.tensor.matmul_mx(out=acc[:], lhsT=on_xo[0], lhsT_scale=on_xo[1],
-                                rhs=xo_codes[:].bitcast(E4M3), rhs_scale=xo_sc[:], start=False, stop=True)
+        xt_side = (xt_codes[:].bitcast(E5M2), xt_sc[:])
+        xo_side = (xo_codes[:].bitcast(E4M3), xo_sc[:])
+
+        def product(acc, t, with_w, with_w2):
+            nc.tensor.matmul_mx(out=acc[:], lhsT=w_codes[:, 2 * P * t : 2 * P * (t + 1)].bitcast(E2M1), lhsT_scale=w_sc[:, t, :],
+                                rhs=with_w[0], rhs_scale=with_w[1], start=True, stop=False)
+            nc.tensor.matmul_mx(out=acc[:], lhsT=w2_codes[:, P * t : P * (t + 1)].bitcast(E5M2), lhsT_scale=w2_sc[:, t, :],
+                                rhs=with_w2[0], rhs_scale=with_w2[1], start=False, stop=True)
 
         pw_read = keep.tile([P, PACK, O], F32)
         last = PACK - 1
@@ -150,8 +156,8 @@ def tile_list_crossed_twoboards_one_finalgate_kernel(
         for t in range(PACK):
             a_acc = psum.tile([P, J], F32, name="a_acc")
             b_acc = psum.tile([P, J], F32, name="b_acc")
-            product(a_acc, t, True)
-            product(b_acc, t, False)
+            product(a_acc, t, xt_side, xo_side)
+            product(b_acc, t, xo_side, xt_side)
             a_sb = keep.tile([P, J], F32, name=f"a_sb{t}")
             b_sb = keep.tile([P, J], F32, name=f"b_sb{t}")
             nc.vector.tensor_copy(out=a_sb[:], in_=a_acc[:])

@@ -88,7 +88,7 @@ def tile_list_crossed_twoboards_one_finalgate_kernel(
         pw = [keep.tile([P, C], F32, name=f"pw{t}") for t in range(PACK)]
         pv = [keep.tile([P, C], F32, name=f"pv{t}") for t in range(PACK)]
         for t in range(PACK):
-            engine = nc.vector if t == 0 else nc.gpsimd
+            engine = nc.vector if t < PACK // 2 else nc.gpsimd
             engine.memset(pw[t][:].bitcast(I32), 0)
             engine.memset(pv[t][:].bitcast(I32), 0)
 
@@ -103,18 +103,18 @@ def tile_list_crossed_twoboards_one_finalgate_kernel(
 
         def deal_scales(dealt, plane, t0, t1):
             nc.vector.tensor_copy(
-                out=dealt[:, t0:t1, :].rearrange("p t m -> p m t"),
-                in_=plane[:].rearrange("p (m t) -> p m t", t=PACK)[:, :, t0:t1],
+                out=dealt[:, t0:t1, :],
+                in_=plane[:].rearrange("p (m t) -> p t m", t=PACK)[:, t0:t1, :],
             )
 
         nc.scalar.copy(
-            out=w_codes[:].bitcast(U16).rearrange("p (t m) -> p m t", t=PACK),
-            in_=w_raw[:].bitcast(U16).rearrange("p (m t) -> p m t", t=PACK),
+            out=w_codes[:].bitcast(U16).rearrange("p (t m) -> p t m", t=PACK),
+            in_=w_raw[:].bitcast(U16).rearrange("p (m t) -> p t m", t=PACK),
         )
         for t0, t1 in ((0, 1), (1, PACK)):
             nc.scalar.copy(
-                out=w2_codes[:].rearrange("p (t m) -> p m t", t=PACK)[:, :, t0:t1],
-                in_=w2_raw[:].bitcast(U32).rearrange("p (m t) -> p m t", t=PACK)[:, :, t0:t1],
+                out=w2_codes[:].rearrange("p (t m) -> p t m", t=PACK)[:, t0:t1, :],
+                in_=w2_raw[:].bitcast(U32).rearrange("p (m t) -> p t m", t=PACK)[:, t0:t1, :],
             )
         nc.vector.tensor_copy(xt_codes[:], xt_tab[:].bitcast(U32).indirect(l_xt[:]))
         nc.vector.tensor_copy(xt_sc[:], xt_plane[:].indirect(l_xt[:]))

from contextlib import ExitStack

import concourse.mybir as mybir

K, T, Z, J, R, C, O, N, E = 512, 1024, 1024, 256, 512, 512, 256, 256, 1024
FLOPS = 2 * (4 * K * R * J + R * N * O)

F32 = mybir.dt.float32
BF16 = mybir.dt.bfloat16
I32 = mybir.dt.int32
U32 = mybir.dt.uint32
U16 = mybir.dt.uint16
U8 = mybir.dt.uint8
E4M3 = mybir.dt.float8_e4m3fn_x4
E5M2 = mybir.dt.float8_e5m2_x4
E2M1 = mybir.dt.float4_e2m1fn_x4
ACT = mybir.ActivationFunctionType
ALU = mybir.AluOpType

P = 128
PACK = 4
HALF = O // 2
LINE = 4


def load_scales(queue, plane, scales, quadrants=(0, 1, 2, 3)):
    for q in quadrants:
        queue.dma_start(out=plane[32 * q : 32 * q + 4, :].bitcast(I32), in_=scales[0, 4 * q : 4 * q + 4, :].bitcast(I32))


def tile_list_crossed_twoboards_one_finalgate_kernel(
    tc, xt_words, xt_scales, xo_words, xo_scales, w_words, w_scales, w2_words, w2_scales, wb_words, wb_scales,
    tz, so, bo, offs, offs2, offs3, offs4, offs5, offs6, offs7, out,
):
    nc = tc.nc
    with ExitStack() as ctx:
        lists = ctx.enter_context(tc.tile_pool(name="lists", bufs=1))
        keep = ctx.enter_context(tc.tile_pool(name="keep", bufs=1))
        psum = ctx.enter_context(tc.psum_pool(name="psum", bufs=2))

        def load_list(src, name):
            tile = lists.tile([P, J // 16], U16, name=name)
            nc.sync.dma_start(tile[:], src)
            return tile

        xt_plane = keep.tile([P, T], U8, align_bytes=64)
        xo_plane = keep.tile([P, Z], U8, align_bytes=64)
        w_plane = keep.tile([P, R], U8, align_bytes=64)
        w2_plane = keep.tile([P, R], U8, align_bytes=64)
        wb_plane = keep.tile([P, N], U8, align_bytes=64)
        nc.gpsimd.memset(xt_plane[:].bitcast(I32), 0)
        nc.vector.memset(xo_plane[:].bitcast(I32), 0)
        nc.gpsimd.memset(w_plane[:].bitcast(I32), 0)
        nc.vector.memset(w2_plane[:].bitcast(I32), 0)
        nc.gpsimd.memset(wb_plane[:].bitcast(I32), 0)
        warm_in = keep.tile([P, 1], F32)
        warm_out = keep.tile([P, 1], F32)
        nc.gpsimd.memset(warm_in[:], 0.0)
        nc.scalar.activation(out=warm_out[:], in_=warm_in[:], func=ACT.Sigmoid)

        xt_tab = keep.tile([P, T], I32, align_bytes=64, tag="xt_tab_then_tz")
        xo_tab = keep.tile([P, Z], I32, align_bytes=64, tag="xo_tab_then_tz")
        w_raw = keep.tile([P, 2 * R], U8, align_bytes=64)
        w2_raw = keep.tile([P, R], I32, align_bytes=64)
        l_xt = load_list(offs, "l_xt")
        l_xo = load_list(offs2, "l_xo")
        load_scales(nc.sync, xt_plane, xt_scales, (0, 1, 2, 3,))
        load_scales(nc.sync, w_plane, w_scales, (0,))
        nc.gpsimd.dma_start(out=w_raw[:].bitcast(I32), in_=w_words[0].bitcast(I32))
        load_scales(nc.gpsimd, w_plane, w_scales, (3,))
        nc.sync.dma_start(out=xt_tab[:], in_=xt_words[0].rearrange("p n t -> p (n t)").bitcast(I32))
        load_scales(nc.sync, xo_plane, xo_scales)
        load_scales(nc.sync, w_plane, w_scales, (1, 2))
        nc.sync.dma_start(out=xo_tab[:], in_=xo_words[0].rearrange("p n t -> p (n t)").bitcast(I32))
        nc.sync.dma_start(out=w2_raw[:], in_=w2_words[0].rearrange("p n t -> p (n t)").bitcast(I32))
        load_scales(nc.sync, w2_plane, w2_scales, (0, 1, 2, 3,))
        l_pw_put = load_list(offs3, "l_pw_put")
        l_pv_put = load_list(offs4, "l_pv_put")
        l_pw_get = load_list(offs5, "l_pw_get")
        l_pv_get = load_list(offs6, "l_pv_get")
        l_tz = load_list(offs7, "l_tz")
        slope = keep.tile([P, N // P], F32)
        offset = keep.tile([P, N // P], F32)
        with nc.allow_non_contiguous_dma(reason="one value a partition"):
            nc.sync.dma_start(out=slope[:], in_=so.rearrange("(c p) o -> p (c o)", p=P))
            nc.sync.dma_start(out=offset[:], in_=bo.rearrange("(c p) o -> p (c o)", p=P))

        pw = [keep.tile([P, C], F32, name=f"pw{t}") for t in range(PACK)]
        pv = [keep.tile([P, C], F32, name=f"pv{t}") for t in range(PACK)]
        for t in range(PACK):
            engine = nc.vector if t < PACK // 2 else nc.gpsimd
            engine.memset(pw[t][:].bitcast(I32), 0)
            engine.memset(pv[t][:].bitcast(I32), 0)

        xt_codes = keep.tile([P, J], U32, align_bytes=64)
        xt_sc = keep.tile([P, J], U8, align_bytes=64)
        xo_codes = keep.tile([P, J], U32, align_bytes=64)
        xo_sc = keep.tile([P, J], U8, align_bytes=64)
        w_codes = keep.tile([P, 2 * R], U8, align_bytes=64)
        w2_codes = keep.tile([P, R], U32, align_bytes=64)
        w_sc = keep.tile([P, PACK, P], U8, align_bytes=64)
        w2_sc = keep.tile([P, PACK, P], U8, align_bytes=64)

        def deal_scales(dealt, plane, t0, t1):
            nc.vector.tensor_copy(
                out=dealt[:, t0:t1, :],
                in_=plane[:].rearrange("p (m t) -> p t m", t=PACK)[:, t0:t1, :],
            )

        nc.scalar.copy(
            out=w_codes[:].bitcast(U16).rearrange("p (t m) -> p t m", t=PACK),
            in_=w_raw[:].bitcast(U16).rearrange("p (m t) -> p t m", t=PACK),
        )
        for t0, t1 in ((0, 1), (1, PACK)):
            nc.scalar.copy(
                out=w2_codes[:].rearrange("p (t m) -> p t m", t=PACK)[:, t0:t1, :],
                in_=w2_raw[:].bitcast(U32).rearrange("p (m t) -> p t m", t=PACK)[:, t0:t1, :],
            )
        nc.vector.tensor_copy(xt_codes[:], xt_tab[:].bitcast(U32).indirect(l_xt[:]))
        nc.vector.tensor_copy(xt_sc[:], xt_plane[:].indirect(l_xt[:]))
        nc.vector.tensor_copy(xo_sc[:], xo_plane[:].indirect(l_xo[:]))
        deal_scales(w_sc, w_plane, 0, PACK)
        nc.vector.tensor_copy(xo_codes[:], xo_tab[:].bitcast(U32).indirect(l_xo[:]))
        deal_scales(w2_sc, w2_plane, 0, 1)
        deal_scales(w2_sc, w2_plane, 1, PACK)
        tz_rows = []
        for c, tag in enumerate(("xt_tab_then_tz", "xo_tab_then_tz")):
            rows = keep.tile([P, E], F32, name=f"tz_rows{c}", align_bytes=64, tag=tag)
            nc.sync.dma_start(out=rows[:], in_=tz[c * P : (c + 1) * P, :])
            tz_rows.append(rows)

        wb_codes = keep.tile([P, 2 * N], U8, align_bytes=64)
        nc.sync.dma_start(out=wb_codes[:].bitcast(I32), in_=wb_words[0].bitcast(I32))
        load_scales(nc.sync, wb_plane, wb_scales)

        xt_side = (xt_codes[:].bitcast(E5M2), xt_sc[:])
        xo_side = (xo_codes[:].bitcast(E4M3), xo_sc[:])

        def product(acc, t, with_w, with_w2):
            nc.tensor.matmul_mx(out=acc[:], lhsT=w_codes[:, 2 * P * t : 2 * P * (t + 1)].bitcast(E2M1), lhsT_scale=w_sc[:, t, :],
                                rhs=with_w[0], rhs_scale=with_w[1], start=True, stop=False)
            nc.tensor.matmul_mx(out=acc[:], lhsT=w2_codes[:, P * t : P * (t + 1)].bitcast(E5M2), lhsT_scale=w2_sc[:, t, :],
                                rhs=with_w2[0], rhs_scale=with_w2[1], start=False, stop=True)

        pw_read = keep.tile([P, PACK, O], F32)
        last = PACK - 1
        halves = [(h * HALF, (h + 1) * HALF) for h in range(2)]

        def read_pw(t):
            nc.scalar.activation(out=pw_read[:, t, :], in_=pw[t][:].indirect(l_pw_get[:]), func=ACT.Copy)

        def subtract(t, o0, o1):
            nc.vector.tensor_tensor(diff[:, t, o0:o1], pv[t][:].indirect(l_pv_get[:, o0 // 16 : o1 // 16]),
                                    pw_read[:, t, o0:o1], ALU.subtract)

        for t in range(PACK):
            a_acc = psum.tile([P, J], F32, name="a_acc")
            b_acc = psum.tile([P, J], F32, name="b_acc")
            product(a_acc, t, xt_side, xo_side)
            product(b_acc, t, xo_side, xt_side)
            a_sb = keep.tile([P, J], F32, name=f"a_sb{t}")
            b_sb = keep.tile([P, J], F32, name=f"b_sb{t}")
            nc.vector.tensor_copy(out=a_sb[:], in_=a_acc[:])
            nc.scalar.copy(out=b_sb[:], in_=b_acc[:])
            if t >= 1:
                read_pw(t - 1)
            if t == 2:
                diff = keep.tile([P, PACK, O], F32, tag="b_sb1")
            if t >= 2:
                subtract(t - 2, 0, O)
            nc.scalar.activation(out=pw[t][:].indirect(l_pw_put[:]), in_=a_sb[:], func=ACT.Copy)
            nc.vector.tensor_copy(out=pv[t][:].indirect(l_pv_put[:]), in_=b_sb[:])

        def make_gate(c, tag):
            gate = keep.tile([P, O], F32, name=f"gate{c}", tag=tag)
            nc.scalar.activation(out=gate[:], in_=tz_rows[c][:].indirect(l_tz[:]), func=ACT.Sigmoid,
                                 bias=offset[:, c : c + 1], scale=slope[:, c : c + 1])
            return gate

        mag = keep.tile([P, PACK, O], BF16, tag=f"a_sb{last}")
        nc.scalar.activation(out=mag[:, : last - 1, :], in_=diff[:, : last - 1, :], func=ACT.Abs)
        subtract(last - 1, 0, O)
        nc.scalar.activation(out=mag[:, last - 1, :], in_=diff[:, last - 1, :], func=ACT.Abs)
        for o0, o1 in halves:
            nc.vector.tensor_copy(pw_read[:, last, o0:o1], pw[last][:].indirect(l_pw_get[:, o0 // 16 : o1 // 16]))
        gates = [make_gate(0, f"b_sb{last}")]
        for o0, o1 in halves:
            subtract(last, o0, o1)
            nc.scalar.activation(out=mag[:, last, o0:o1], in_=diff[:, last, o0:o1], func=ACT.Abs)
        gates.append(make_gate(1, "b_sb1"))
        hid = []
        for h, (o0, o1) in enumerate(halves):
            hid_h = keep.tile([P, HALF * PACK], BF16, name=f"hid{h}", align_bytes=64)
            nc.vector.tensor_copy(out=hid_h[:].rearrange("p (o t) -> p o t", t=PACK),
                                  in_=mag[:, :, o0:o1].rearrange("p t o -> p o t"))
            hid.append(hid_h)
        out_rows = out.rearrange("(c p) o -> p c o", p=P)
        for h, (o0, o1) in enumerate(halves):
            hid_codes = keep.tile([P, HALF], U32, name=f"hid_codes{h}", align_bytes=64)
            hid_sc = keep.tile([P, HALF], U8, name=f"hid_sc{h}", align_bytes=64)
            nc.vector.quantize_mx(out=hid_codes[:].bitcast(E4M3), scales=hid_sc[:], in_=hid[h][:])
            p_acc = psum.tile([P, N // P, HALF], F32, name="p_acc")
            for c in range(N // P):
                nc.tensor.matmul_mx(out=p_acc[:, c, :], lhsT=wb_codes[:, 2 * P * c : 2 * P * (c + 1)].bitcast(E2M1),
                                    lhsT_scale=wb_plane[:, P * c : P * (c + 1)],
                                    rhs=hid_codes[:].bitcast(E4M3), rhs_scale=hid_sc[:], start=True, stop=True)
            y = keep.tile([P, N // P, HALF], F32, name=f"y{h}")
            for c in range(N // P):
                nc.vector.tensor_tensor(y[:, c, :], p_acc[:, c, :], gates[c][:, o0:o1], ALU.mult)
            nc.sync.dma_start(out=out_rows[:, :, o0:o1], in_=y[:])
